import numpy as np
import ml_dtypes


def mxq(x, axis, fmt="e4m3"):
    dtype, down = {"e4m3": (ml_dtypes.float8_e4m3fn, 7), "e5m2": (ml_dtypes.float8_e5m2, 14)}[fmt]
    v = np.moveaxis(np.asarray(x, np.float32).astype(ml_dtypes.bfloat16).astype(np.float64), axis, -1)
    blocks = v.reshape(v.shape[:-1] + (-1, 32))
    amax = np.abs(blocks).max(-1, keepdims=True)
    byte = np.maximum(np.where(amax > 0, np.frexp(amax)[1] - 1 + 127, 0) - down, 1)
    scale = np.exp2(byte - 127.0)
    codes = (blocks / scale).astype(np.float32).astype(dtype).astype(np.float64)
    return np.moveaxis((codes * scale).reshape(v.shape), -1, axis)


WIDE = False


def mx_kscale(k):
    if not WIDE:
        return np.ones(k)
    levels = np.array([10, -10, 5, -5, 0])
    if k % 512:
        return np.exp2(np.random.permutation(np.resize(levels, k // 32))).repeat(32)
    a = np.empty((k // 512, 16))
    for p in range(k // 512):
        a[p, :8] = np.random.permutation(np.resize(levels, 8))
        for g in range(8):
            far = levels[np.abs(levels - a[p, g]) >= 10]
            a[p, g + 8] = far[np.random.randint(len(far))]
    return np.exp2(a.ravel()).repeat(32)


def f64(x):
    return np.asarray(x).astype(np.float64)


def striped(idx):
    return np.tile(idx.reshape(-1, 16).T, (8, 1)).astype(np.uint16)


def unstriped(offs):
    return offs[:16].T.reshape(-1).astype(np.int64)


def striped8(idx):
    return np.concatenate([x.reshape(-1, 16).T for x in idx]).astype(np.uint16)


def runs(offs, k):
    lists = np.stack([offs[16 * r : 16 * r + 16].T.reshape(-1) for r in range(8)]).astype(np.int64)
    return lists[np.arange(k) % 512 // 64]


def pack_weight(w):
    k, n = w.shape
    w = f64(np.asarray(w, np.float32).astype(ml_dtypes.bfloat16)).reshape(k // 32, 32, n)
    amax = np.abs(w).max(1)
    byte = np.clip(np.where(amax > 0, np.frexp(amax)[1] - 1 + 127 - 7, 1), 1, 254)
    scaled = (w * np.exp2(127.0 - byte)[:, None, :]).reshape(k, n).astype(np.float32)
    words = np.ascontiguousarray(scaled.reshape(k // 512, 128, 4, n).transpose(0, 1, 3, 2)).astype(ml_dtypes.float8_e4m3fn).view(np.uint8)
    return words, np.ascontiguousarray(byte.astype(np.uint8).reshape(k // 512, 16, n))


def unpack_weight(words, scales):
    g, p, n, _ = words.shape
    vals = np.ascontiguousarray(words).view(ml_dtypes.float8_e4m3fn).astype(np.float64) * np.repeat(np.exp2(scales.astype(np.float64) - 127.0), 8, axis=1)[..., None]
    return vals.transpose(0, 1, 3, 2).reshape(g * 512, n)


def relu(v):
    return np.maximum(v, 0.0)


K, T, S, G, H = 512, 2048, 512, 2048, 512


def setup_inputs():
    n = np.random.standard_normal
    s = mx_kscale(K)[:, None]
    packed_xT = pack_weight(n((K, T)) * s)
    packed_dT = pack_weight(n((K, G)) / s)
    return {
        "x_words": packed_xT[0],
        "x_scales": packed_xT[1],
        "d_words": packed_dT[0],
        "d_scales": packed_dT[1],
        "gs": (np.random.uniform(0.5, 1.5, (K, 1)) * s).astype(np.float32),
        "offs": striped(np.random.permutation(T)[:S]),
        "k1": striped8(np.random.randint(0, G, (8, H))),
        "k2": striped8(np.random.randint(0, G, (8, H))),
        "k3": striped8(np.random.randint(0, G, (8, H))),
        "k4": striped8(np.random.randint(0, G, (8, H))),
    }


def reference(x_words, x_scales, d_words, d_scales, gs, offs, k1, k2, k3, k4):
    d_k3 = unpack_weight(d_words, d_scales)[np.arange(K)[:, None], runs(k3, K)]
    d_k1 = unpack_weight(d_words, d_scales)[np.arange(K)[:, None], runs(k1, K)]
    xq = unpack_weight(x_words, x_scales)[:, unstriped(offs)]
    d_k2 = unpack_weight(d_words, d_scales)[np.arange(K)[:, None], runs(k2, K)]
    h = relu(0.0625 * ((d_k1.T @ xq) + 0.25 * (d_k2.T @ xq)))
    z = f64(gs) * h
    zq = mxq(z, 0, "e4m3")
    d_k4 = unpack_weight(d_words, d_scales)[np.arange(K)[:, None], runs(k4, K)]
    return 0.0625 * ((d_k3.T @ zq) + 0.25 * (d_k4.T @ zq))

@@ -1,0 +1,179 @@
+from contextlib import ExitStack
+
+import concourse.mybir as mybir
+from concourse.masks import make_identity
+
+K, T, S, G, H = 512, 2048, 512, 2048, 512
+FLOPS = 4 * 2 * K * H * S
+
+F32 = mybir.dt.float32
+BF16 = mybir.dt.bfloat16
+I32 = mybir.dt.int32
+U32 = mybir.dt.uint32
+U16 = mybir.dt.uint16
+U8 = mybir.dt.uint8
+FP8X4 = mybir.dt.float8_e4m3fn_x4
+ALU = mybir.AluOpType
+COPY = mybir.ActivationFunctionType.Copy
+
+P = 128
+PACK = 4
+CHUNKS = S // P
+HALF = S // 2
+
+
+def tile_picked_pqres2_relu_p_kernel(
+    tc, x_words, x_scales, d_words, d_scales, gs, offs, k1, k2, k3, k4, out
+):
+    nc = tc.nc
+    with ExitStack() as ctx:
+        sb = ctx.enter_context(tc.tile_pool(name="sb", bufs=1))
+        shared = ctx.enter_context(tc.tile_pool(name="shared", bufs=1))
+        psum = ctx.enter_context(tc.psum_pool(name="psum", bufs=1))
+
+        def load_list(name, src):
+            tile = sb.tile([P, S // 16], U16, name=name)
+            nc.sync.dma_start(tile[:], src)
+            return tile
+
+        def load_scales(name, src):
+            tile = sb.tile([P, T], U8, name=name, align_bytes=64)
+            rows = src[0].bitcast(I32)
+            nc.sync.dma_start(tile[:].bitcast(I32), rows.unsqueeze(1).to_broadcast([16, 8, T // 4]))
+            return tile
+
+        def load_words(name, src, pool, **place):
+            tile = pool.tile([P, T], I32, name=name, align_bytes=64, **place)
+            nc.sync.dma_start(tile[:], src[0].rearrange("p n t -> p (n t)").bitcast(I32))
+            return tile
+
+        k1_t = load_list("k1_t", k1)
+        ds_t = load_scales("ds_t", d_scales)
+        offs_t = load_list("offs_t", offs)
+        xs_t = load_scales("xs_t", x_scales)
+        k2_t = load_list("k2_t", k2)
+        dw_t = load_words("dw_t", d_words, sb)
+        xw_t = load_words("xw_t", x_words, shared, offset=0)
+        k3_t = load_list("k3_t", k3)
+        k4_t = load_list("k4_t", k4)
+        gs_t = sb.tile([P, PACK], F32, name="gs_t")
+        nc.sync.dma_start(gs_t[:], gs.rearrange("(p t) o -> p (t o)", t=PACK))
+
+        ident = sb.tile([P, P], F32, name="ident", align_bytes=64)
+        make_identity(nc, ident[:])
+        gain = sb.tile([P, PACK], F32, name="gain")
+        nc.scalar.activation(gain[:], gs_t[:], COPY, scale=0.0625)
+
+        def gather_planes(name, picks, pool, **place):
+            n = len(picks)
+            picked = pool.tile([P, n * S], U8, name=name + "_picked", align_bytes=64, **place)
+            planes = sb.tile([P, n * S], U8, name=name + "_planes", align_bytes=64)
+            nc.gpsimd.memset(planes[:].bitcast(I32), 0)
+            for i, (table, lst) in enumerate(picks):
+                nc.vector.tensor_copy(picked[:, i * S : (i + 1) * S], table[:].indirect(lst[:]))
+            for r in range(4):
+                nc.sync.dma_start(
+                    planes[:].bitcast(I32)[r:P:32, :], picked[:].bitcast(I32)[8 * r : P : 32, :]
+                )
+            return [planes[:, i * S : (i + 1) * S] for i in range(n)]
+
+        def gather_words(name, table, lst, pool, **place):
+            tile = pool.tile([P, S], U32, name=name, align_bytes=64, **place)
+            nc.vector.tensor_copy(tile[:], table[:].bitcast(U32).indirect(lst[:]))
+            return tile
+
+        s1, sx, s2 = gather_planes("first", [(ds_t, k1_t), (xs_t, offs_t), (ds_t, k2_t)], sb)
+        w1 = gather_words("w1", dw_t, k1_t, sb)
+        w2 = gather_words("w2", dw_t, k2_t, sb)
+        wx = sb.tile([P, S], U32, name="wx", align_bytes=64)
+        for h in range(2):
+            nc.vector.tensor_copy(
+                wx[:, h * HALF : (h + 1) * HALF],
+                xw_t[:].bitcast(U32).indirect(offs_t[:, h * HALF // 16 : (h + 1) * HALF // 16]),
+            )
+        s3, s4 = gather_planes("second", [(ds_t, k3_t), (ds_t, k4_t)], shared, offset=6144)
+        w3 = gather_words("w3", dw_t, k3_t, shared, offset=2048)
+        w4 = gather_words("w4", dw_t, k4_t, shared, offset=4096)
+
+        def mx(acc, lw, ls, rw, rs):
+            nc.tensor.matmul_mx(
+                out=acc, lhsT=lw.bitcast(FP8X4), lhsT_scale=ls, rhs=rw.bitcast(FP8X4), rhs_scale=rs,
+                start=True, stop=True,
+            )
+
+        parts = {}
+        for c in range(CHUNKS):
+            for name, w, s, first_bank, scale in (("a", w1, s1, 0, 1.0), ("b", w2, s2, 4, 0.25)):
+                toks = slice(c * P, (c + 1) * P)
+                acc = psum.tile([P, H], F32, name=f"{name}{c}", tag=f"bank{first_bank + c}")
+                mx(acc[:], wx[:, toks], sx[:, toks], w[:], s)
+                parts[name, c] = (acc, scale)
+
+        dealt = {}
+        pre = {}
+        z_bf = {}
+        z_mx = {}
+        sums = {}
+
+        def deal(name, c):
+            acc, scale = parts[name, c]
+            tile = sb.tile([P, PACK, P], F32, name=f"{name}{c}_sb", tag=f"{name}{c}_sb", align_bytes=64)
+            nc.scalar.activation(tile[:], acc[:].rearrange("p (m t) -> p t m", t=PACK), COPY, scale=scale)
+            dealt[name, c] = tile
+
+        def turn(c):
+            pre[c] = psum.tile([P, PACK, P], F32, name=f"pre{c}", tag=f"bank{c}")
+            for t in range(PACK):
+                nc.tensor.matmul(pre[c][:, t, :], dealt["a", c][:, t, :], ident[:], start=True, stop=False, is_transpose=True)
+                nc.tensor.matmul(pre[c][:, t, :], dealt["b", c][:, t, :], ident[:], start=False, stop=True, is_transpose=True)
+
+        def weigh(c):
+            tag = ("b2_sb", "a2_sb", "z_bf2", "z_bf3")[c]
+            z_bf[c] = sb.tile([P, P, PACK], BF16, name=f"z_bf{c}", tag=tag, align_bytes=64)
+            nc.vector.scalar_tensor_tensor(
+                out=z_bf[c][:],
+                in0=pre[c][:].rearrange("p t j -> p j t"),
+                scalar=0.0,
+                in1=gain[:].unsqueeze(1).to_broadcast([P, P, PACK]),
+                op0=ALU.max,
+                op1=ALU.mult,
+            )
+
+        def quantise(c):
+            z_w = sb.tile([P, P], U32, name=f"z_w{c}", align_bytes=64)
+            z_s = sb.tile([P, P], U8, name=f"z_s{c}", align_bytes=64)
+            nc.vector.quantize_mx(out=z_w[:].bitcast(FP8X4), scales=z_s[:], in_=z_bf[c][:].rearrange("p j t -> p (j t)"))
+            z_mx[c] = (z_w, z_s)
+
+        def second(c):
+            z_w, z_s = z_mx[c]
+            coarse = psum.tile([P, CHUNKS, P], F32, name=f"coarse{c}", tag=f"bank{c}")
+            fine = psum.tile([P, CHUNKS, P], F32, name=f"fine{c}", tag=f"bank{4 + c}")
+            for acc, w, s in ((fine, w4, s4), (coarse, w3, s3)):
+                for i in range(CHUNKS):
+                    rows = slice(i * P, (i + 1) * P)
+                    mx(acc[:, i, :], w[:, rows], s[:, rows], z_w[:], z_s[:])
+            fine_sb = sb.tile([P, CHUNKS, P], F32, name=f"fine{c}_sb")
+            nc.scalar.activation(fine_sb[:], fine[:], COPY, scale=0.015625)
+            sums[c] = (coarse, fine_sb)
+
+        def finish(c):
+            coarse, fine_sb = sums[c]
+            res = sb.tile([P, CHUNKS, P], F32, name=f"res{c}")
+            nc.vector.scalar_tensor_tensor(
+                out=res[:], in0=coarse[:], scalar=0.0625, in1=fine_sb[:], op0=ALU.mult, op1=ALU.add
+            )
+            nc.sync.dma_start(out[:, c * P : (c + 1) * P].rearrange("(i p) j -> p i j", p=P), res[:])
+
+        for c in range(CHUNKS):
+            deal("a", c)
+            deal("b", c)
+            turn(c)
+        for c in range(CHUNKS + 1):
+            if c < CHUNKS:
+                weigh(c)
+            if c > 0:
+                quantise(c - 1)
+                second(c - 1)
+        for c in range(CHUNKS):
+            finish(c)

@@ -84,13 +84,8 @@ def tile_picked_pqres2_relu_p_kernel(
 
         s1, sx, s2 = gather_planes("first", [(ds_t, k1_t), (xs_t, offs_t), (ds_t, k2_t)], sb)
         w1 = gather_words("w1", dw_t, k1_t, sb)
-        w2 = gather_words("w2", dw_t, k2_t, sb)
-        wx = sb.tile([P, S], U32, name="wx", align_bytes=64)
-        for h in range(2):
-            nc.vector.tensor_copy(
-                wx[:, h * HALF : (h + 1) * HALF],
-                xw_t[:].bitcast(U32).indirect(offs_t[:, h * HALF // 16 : (h + 1) * HALF // 16]),
-            )
+        wx = gather_words("wx", xw_t, offs_t, sb)
+        w2 = gather_words("w2", dw_t, k2_t, shared, offset=0)
         s3, s4 = gather_planes("second", [(ds_t, k3_t), (ds_t, k4_t)], shared, offset=6144)
         w3 = gather_words("w3", dw_t, k3_t, shared, offset=2048)
         w4 = gather_words("w4", dw_t, k4_t, shared, offset=4096)
@@ -102,8 +97,10 @@ def tile_picked_pqres2_relu_p_kernel(
             )
 
         parts = {}
-        for c in range(CHUNKS):
-            for name, w, s, first_bank, scale in (("a", w1, s1, 0, 1.0), ("b", w2, s2, 4, 0.25)):
+        order = [("a", 0), ("a", 1), ("b", 0), ("b", 1), ("a", 2), ("b", 2), ("a", 3), ("b", 3)]
+        for name, c in order:
+            w, s, first_bank, scale = {"a": (w1, s1, 0, 1.0), "b": (w2, s2, 4, 0.25)}[name]
+            if True:
                 toks = slice(c * P, (c + 1) * P)
                 acc = psum.tile([P, H], F32, name=f"{name}{c}", tag=f"bank{first_bank + c}")
                 mx(acc[:], wx[:, toks], sx[:, toks], w[:], s)
@@ -160,14 +157,19 @@ def tile_picked_pqres2_relu_p_kernel(
         def finish(c):
             coarse, fine_sb = sums[c]
             res = sb.tile([P, CHUNKS, P], F32, name=f"res{c}")
-            nc.vector.scalar_tensor_tensor(
-                out=res[:], in0=coarse[:], scalar=0.0625, in1=fine_sb[:], op0=ALU.mult, op1=ALU.add
-            )
-            nc.sync.dma_start(out[:, c * P : (c + 1) * P].rearrange("(i p) j -> p i j", p=P), res[:])
+            dst = out[:, c * P : (c + 1) * P].rearrange("(i p) j -> p i j", p=P)
+            step = CHUNKS // 2 if c == CHUNKS - 1 else CHUNKS
+            for i in range(0, CHUNKS, step):
+                part = slice(i, i + step)
+                nc.vector.scalar_tensor_tensor(
+                    out=res[:, part, :], in0=coarse[:, part, :], scalar=0.0625, in1=fine_sb[:, part, :],
+                    op0=ALU.mult, op1=ALU.add,
+                )
+                nc.sync.dma_start(dst[:, part, :], res[:, part, :])
 
+        for name, c in order:
+            deal(name, c)
         for c in range(CHUNKS):
-            deal("a", c)
-            deal("b", c)
             turn(c)
         for c in range(CHUNKS + 1):
             if c < CHUNKS:

@@ -125,10 +125,11 @@ def tile_picked_pqres2_relu_p_kernel(
                 nc.tensor.matmul(pre[c][:, t, :], dealt["b", c][:, t, :], ident[:], start=False, stop=True, is_transpose=True)
 
         def weigh(c):
-            tag = ("b2_sb", "a2_sb", "z_bf2", "z_bf3")[c]
-            z_bf[c] = sb.tile([P, P, PACK], BF16, name=f"z_bf{c}", tag=tag, align_bytes=64)
+            h, part = divmod(c, 2)
+            if part == 0:
+                z_bf[h] = sb.tile([P, HALF, PACK], BF16, name=f"z_bf{h}", tag=("b2_sb", "z_bf1")[h], align_bytes=64)
             nc.vector.scalar_tensor_tensor(
-                out=z_bf[c][:],
+                out=z_bf[h][:, part * P : (part + 1) * P, :],
                 in0=pre[c][:].rearrange("p t j -> p j t"),
                 scalar=0.0,
                 in1=gain[:].unsqueeze(1).to_broadcast([P, P, PACK]),
@@ -136,30 +137,27 @@ def tile_picked_pqres2_relu_p_kernel(
                 op1=ALU.mult,
             )
 
-        def quantise(c):
-            z_w = sb.tile([P, P], U32, name=f"z_w{c}", align_bytes=64)
-            z_s = sb.tile([P, P], U8, name=f"z_s{c}", align_bytes=64)
-            nc.vector.quantize_mx(out=z_w[:].bitcast(FP8X4), scales=z_s[:], in_=z_bf[c][:].rearrange("p j t -> p (j t)"))
-            z_mx[c] = (z_w, z_s)
+        def second(h):
+            z_w = sb.tile([P, HALF], U32, name=f"z_w{h}", align_bytes=64)
+            z_s = sb.tile([P, HALF], U8, name=f"z_s{h}", align_bytes=64)
+            nc.vector.quantize_mx(out=z_w[:].bitcast(FP8X4), scales=z_s[:], in_=z_bf[h][:].rearrange("p j t -> p (j t)"))
+            for pair in range(2):
+                coarse = psum.tile([P, 2, HALF], F32, name=f"coarse{h}{pair}", tag=f"bank{2 * h + pair}")
+                fine = psum.tile([P, 2, HALF], F32, name=f"fine{h}{pair}", tag=f"bank{4 + 2 * h + pair}")
+                for acc, w, s in ((fine, w4, s4), (coarse, w3, s3)):
+                    for i in range(2):
+                        rows = slice((2 * pair + i) * P, (2 * pair + i + 1) * P)
+                        mx(acc[:, i, :], w[:, rows], s[:, rows], z_w[:], z_s[:])
+                fine_sb = sb.tile([P, 2, HALF], F32, name=f"fine{h}{pair}_sb")
+                nc.scalar.activation(fine_sb[:], fine[:], COPY, scale=0.015625)
+                sums[h, pair] = (coarse, fine_sb)
 
-        def second(c):
-            z_w, z_s = z_mx[c]
-            coarse = psum.tile([P, CHUNKS, P], F32, name=f"coarse{c}", tag=f"bank{c}")
-            fine = psum.tile([P, CHUNKS, P], F32, name=f"fine{c}", tag=f"bank{4 + c}")
-            for acc, w, s in ((fine, w4, s4), (coarse, w3, s3)):
-                for i in range(CHUNKS):
-                    rows = slice(i * P, (i + 1) * P)
-                    mx(acc[:, i, :], w[:, rows], s[:, rows], z_w[:], z_s[:])
-            fine_sb = sb.tile([P, CHUNKS, P], F32, name=f"fine{c}_sb")
-            nc.scalar.activation(fine_sb[:], fine[:], COPY, scale=0.015625)
-            sums[c] = (coarse, fine_sb)
-
-        def finish(c):
-            coarse, fine_sb = sums[c]
-            res = sb.tile([P, CHUNKS, P], F32, name=f"res{c}")
-            dst = out[:, c * P : (c + 1) * P].rearrange("(i p) j -> p i j", p=P)
-            step = CHUNKS // 2 if c == CHUNKS - 1 else CHUNKS
-            for i in range(0, CHUNKS, step):
+        def finish(h, pair):
+            coarse, fine_sb = sums[h, pair]
+            res = sb.tile([P, 2, HALF], F32, name=f"res{h}{pair}")
+            dst = out[2 * pair * P : (2 * pair + 2) * P, h * HALF : (h + 1) * HALF].rearrange("(i p) j -> p i j", p=P)
+            step = 1 if (h, pair) == (1, 1) else 2
+            for i in range(0, 2, step):
                 part = slice(i, i + step)
                 nc.vector.scalar_tensor_tensor(
                     out=res[:, part, :], in0=coarse[:, part, :], scalar=0.0625, in1=fine_sb[:, part, :],
@@ -170,12 +168,15 @@ def tile_picked_pqres2_relu_p_kernel(
         for name, c in order:
             deal(name, c)
         for c in range(CHUNKS):
+            if c == CHUNKS - 1:
+                warm = psum.tile([P, H], F32, name="warm", tag="bank6")
+                for i in range(3):
+                    mx(warm[:], w3[:, :P], s1[:, :P], w3[:], s1)
             turn(c)
-        for c in range(CHUNKS + 1):
-            if c < CHUNKS:
-                weigh(c)
-            if c > 0:
-                quantise(c - 1)
-                second(c - 1)
-        for c in range(CHUNKS):
-            finish(c)
+        for h in range(2):
+            weigh(2 * h)
+            weigh(2 * h + 1)
+            second(h)
+        for h in range(2):
+            for pair in range(2):
+                finish(h, pair)

from contextlib import ExitStack

import concourse.mybir as mybir
from concourse.masks import make_identity

K, T, S, G, H = 512, 2048, 512, 2048, 512
FLOPS = 4 * 2 * K * H * S

F32 = mybir.dt.float32
BF16 = mybir.dt.bfloat16
I32 = mybir.dt.int32
U32 = mybir.dt.uint32
U16 = mybir.dt.uint16
U8 = mybir.dt.uint8
FP8X4 = mybir.dt.float8_e4m3fn_x4
ALU = mybir.AluOpType
COPY = mybir.ActivationFunctionType.Copy

P = 128
PACK = 4
CHUNKS = S // P
HALF = S // 2


def tile_picked_pqres2_relu_p_kernel(
    tc, x_words, x_scales, d_words, d_scales, gs, offs, k1, k2, k3, k4, out
):
    nc = tc.nc
    with ExitStack() as ctx:
        sb = ctx.enter_context(tc.tile_pool(name="sb", bufs=1))
        shared = ctx.enter_context(tc.tile_pool(name="shared", bufs=1))
        psum = ctx.enter_context(tc.psum_pool(name="psum", bufs=1))

        def load_list(name, src):
            tile = sb.tile([P, S // 16], U16, name=name)
            nc.sync.dma_start(tile[:], src)
            return tile

        def load_scales(name, src):
            tile = sb.tile([P, T], U8, name=name, align_bytes=64)
            rows = src[0].bitcast(I32)
            nc.sync.dma_start(tile[:].bitcast(I32), rows.unsqueeze(1).to_broadcast([16, 8, T // 4]))
            return tile

        def load_words(name, src, pool, **place):
            tile = pool.tile([P, T], I32, name=name, align_bytes=64, **place)
            nc.sync.dma_start(tile[:], src[0].rearrange("p n t -> p (n t)").bitcast(I32))
            return tile

        k1_t = load_list("k1_t", k1)
        ds_t = load_scales("ds_t", d_scales)
        offs_t = load_list("offs_t", offs)
        xs_t = load_scales("xs_t", x_scales)
        k2_t = load_list("k2_t", k2)
        dw_t = load_words("dw_t", d_words, sb)
        xw_t = load_words("xw_t", x_words, shared, offset=0)
        k3_t = load_list("k3_t", k3)
        k4_t = load_list("k4_t", k4)
        gs_t = sb.tile([P, PACK], F32, name="gs_t")
        nc.sync.dma_start(gs_t[:], gs.rearrange("(p t) o -> p (t o)", t=PACK))

        ident = sb.tile([P, P], F32, name="ident", align_bytes=64)
        make_identity(nc, ident[:])
        gain = sb.tile([P, PACK], F32, name="gain")
        nc.scalar.activation(gain[:], gs_t[:], COPY, scale=0.0625)

        def gather_planes(name, picks, pool, **place):
            n = len(picks)
            picked = pool.tile([P, n * S], U8, name=name + "_picked", align_bytes=64, **place)
            planes = sb.tile([P, n * S], U8, name=name + "_planes", align_bytes=64)
            nc.gpsimd.memset(planes[:].bitcast(I32), 0)
            for i, (table, lst) in enumerate(picks):
                nc.vector.tensor_copy(picked[:, i * S : (i + 1) * S], table[:].indirect(lst[:]))
            for r in range(4):
                nc.sync.dma_start(
                    planes[:].bitcast(I32)[r:P:32, :], picked[:].bitcast(I32)[8 * r : P : 32, :]
                )
            return [planes[:, i * S : (i + 1) * S] for i in range(n)]

        def gather_words(name, table, lst, pool, **place):
            tile = pool.tile([P, S], U32, name=name, align_bytes=64, **place)
            nc.vector.tensor_copy(tile[:], table[:].bitcast(U32).indirect(lst[:]))
            return tile

        s1, sx, s2 = gather_planes("first", [(ds_t, k1_t), (xs_t, offs_t), (ds_t, k2_t)], sb)
        w1 = gather_words("w1", dw_t, k1_t, sb)
        wx = gather_words("wx", xw_t, offs_t, sb)
        w2 = gather_words("w2", dw_t, k2_t, shared, offset=0)
        s3, s4 = gather_planes("second", [(ds_t, k3_t), (ds_t, k4_t)], shared, offset=6144)
        w3 = gather_words("w3", dw_t, k3_t, shared, offset=2048)
        w4 = gather_words("w4", dw_t, k4_t, shared, offset=4096)

        def mx(acc, lw, ls, rw, rs):
            nc.tensor.matmul_mx(
                out=acc, lhsT=lw.bitcast(FP8X4), lhsT_scale=ls, rhs=rw.bitcast(FP8X4), rhs_scale=rs,
                start=True, stop=True,
            )

        parts = {}
        order = [("a", 0), ("a", 1), ("b", 0), ("b", 1), ("a", 2), ("b", 2), ("a", 3), ("b", 3)]
        for name, c in order:
            w, s, first_bank, scale = {"a": (w1, s1, 0, 1.0), "b": (w2, s2, 4, 0.25)}[name]
            if True:
                toks = slice(c * P, (c + 1) * P)
                acc = psum.tile([P, H], F32, name=f"{name}{c}", tag=f"bank{first_bank + c}")
                mx(acc[:], wx[:, toks], sx[:, toks], w[:], s)
                parts[name, c] = (acc, scale)

        dealt = {}
        pre = {}
        z_bf = {}
        z_mx = {}
        sums = {}

        def deal(name, c):
            acc, scale = parts[name, c]
            tile = sb.tile([P, PACK, P], F32, name=f"{name}{c}_sb", tag=f"{name}{c}_sb", align_bytes=64)
            nc.scalar.activation(tile[:], acc[:].rearrange("p (m t) -> p t m", t=PACK), COPY, scale=scale)
            dealt[name, c] = tile

        def turn(c):
            pre[c] = psum.tile([P, PACK, P], F32, name=f"pre{c}", tag=f"bank{c}")
            for t in range(PACK):
                nc.tensor.matmul(pre[c][:, t, :], dealt["a", c][:, t, :], ident[:], start=True, stop=False, is_transpose=True)
                nc.tensor.matmul(pre[c][:, t, :], dealt["b", c][:, t, :], ident[:], start=False, stop=True, is_transpose=True)

        def weigh(c):
            h, part = divmod(c, 2)
            if part == 0:
                z_bf[h] = sb.tile([P, HALF, PACK], BF16, name=f"z_bf{h}", tag=("b2_sb", "z_bf1")[h], align_bytes=64)
            nc.vector.scalar_tensor_tensor(
                out=z_bf[h][:, part * P : (part + 1) * P, :],
                in0=pre[c][:].rearrange("p t j -> p j t"),
                scalar=0.0,
                in1=gain[:].unsqueeze(1).to_broadcast([P, P, PACK]),
                op0=ALU.max,
                op1=ALU.mult,
            )

        def second(h):
            z_w = sb.tile([P, HALF], U32, name=f"z_w{h}", align_bytes=64)
            z_s = sb.tile([P, HALF], U8, name=f"z_s{h}", align_bytes=64)
            nc.vector.quantize_mx(out=z_w[:].bitcast(FP8X4), scales=z_s[:], in_=z_bf[h][:].rearrange("p j t -> p (j t)"))
            for pair in range(2):
                coarse = psum.tile([P, 2, HALF], F32, name=f"coarse{h}{pair}", tag=f"bank{2 * h + pair}")
                fine = psum.tile([P, 2, HALF], F32, name=f"fine{h}{pair}", tag=f"bank{4 + 2 * h + pair}")
                for acc, w, s in ((fine, w4, s4), (coarse, w3, s3)):
                    for i in range(2):
                        rows = slice((2 * pair + i) * P, (2 * pair + i + 1) * P)
                        mx(acc[:, i, :], w[:, rows], s[:, rows], z_w[:], z_s[:])
                fine_sb = sb.tile([P, 2, HALF], F32, name=f"fine{h}{pair}_sb")
                nc.scalar.activation(fine_sb[:], fine[:], COPY, scale=0.015625)
                sums[h, pair] = (coarse, fine_sb)

        def finish(h, pair):
            coarse, fine_sb = sums[h, pair]
            res = sb.tile([P, 2, HALF], F32, name=f"res{h}{pair}")
            dst = out[2 * pair * P : (2 * pair + 2) * P, h * HALF : (h + 1) * HALF].rearrange("(i p) j -> p i j", p=P)
            step = 1 if (h, pair) == (1, 1) else 2
            for i in range(0, 2, step):
                part = slice(i, i + step)
                nc.vector.scalar_tensor_tensor(
                    out=res[:, part, :], in0=coarse[:, part, :], scalar=0.0625, in1=fine_sb[:, part, :],
                    op0=ALU.mult, op1=ALU.add,
                )
                nc.sync.dma_start(dst[:, part, :], res[:, part, :])

        for name, c in order:
            deal(name, c)
        for c in range(CHUNKS):
            if c == CHUNKS - 1:
                warm = psum.tile([P, H], F32, name="warm", tag="bank6")
                for i in range(3):
                    mx(warm[:], w3[:, :P], s1[:, :P], w3[:], s1)
            turn(c)
        for h in range(2):
            weigh(2 * h)
            weigh(2 * h + 1)
            second(h)
        for h in range(2):
            for pair in range(2):
                finish(h, pair)
